import numpy as np
import ml_dtypes


def mxq(x, axis, fmt="e4m3"):
    dtype, down = {"e4m3": (ml_dtypes.float8_e4m3fn, 7), "e5m2": (ml_dtypes.float8_e5m2, 14)}[fmt]
    v = np.moveaxis(np.asarray(x, np.float32).astype(ml_dtypes.bfloat16).astype(np.float64), axis, -1)
    blocks = v.reshape(v.shape[:-1] + (-1, 32))
    amax = np.abs(blocks).max(-1, keepdims=True)
    byte = np.maximum(np.where(amax > 0, np.frexp(amax)[1] - 1 + 127, 0) - down, 1)
    scale = np.exp2(byte - 127.0)
    codes = (blocks / scale).astype(np.float32).astype(dtype).astype(np.float64)
    return np.moveaxis((codes * scale).reshape(v.shape), -1, axis)


WIDE = False


def mx_kscale(k):
    if not WIDE:
        return np.ones(k)
    levels = np.array([10, -10, 5, -5, 0])
    if k % 512:
        return np.exp2(np.random.permutation(np.resize(levels, k // 32))).repeat(32)
    a = np.empty((k // 512, 16))
    for p in range(k // 512):
        a[p, :8] = np.random.permutation(np.resize(levels, 8))
        for g in range(8):
            far = levels[np.abs(levels - a[p, g]) >= 10]
            a[p, g + 8] = far[np.random.randint(len(far))]
    return np.exp2(a.ravel()).repeat(32)


def f64(x):
    return np.asarray(x).astype(np.float64)


def striped(idx):
    return np.tile(np.asarray(idx).reshape(-1, 16).T, (8, 1)).astype(np.uint16)


def unstriped(offs):
    return offs[:16].T.reshape(-1).astype(np.int64)


E2M1 = np.array([0.0, 0.5, 1.0, 1.5, 2.0, 3.0, 4.0, 6.0, -0.0, -0.5, -1.0, -1.5, -2.0, -3.0, -4.0, -6.0])


def pack_weight(w, fmt):
    k, n = w.shape
    w = f64(np.asarray(w, np.float32).astype(ml_dtypes.bfloat16)).reshape(k // 32, 32, n)
    amax = np.abs(w).max(1)
    if fmt == "e4m3":
        byte = np.frexp(amax)[1] - 1 + 127 - 7
    else:
        mant, ex = np.frexp(amax / 6.0)
        byte = np.where(mant > 0.5, ex, ex - 1) + 127
    byte = np.clip(np.where(amax > 0, byte, 1), 1, 254)
    scaled = (w * np.exp2(127.0 - byte)[:, None, :]).reshape(k, n).astype(np.float32)
    by_word = np.ascontiguousarray(scaled.reshape(k // 512, 128, 4, n).transpose(0, 1, 3, 2))
    if fmt == "e4m3":
        words = by_word.astype(ml_dtypes.float8_e4m3fn).view(np.uint8)
    else:
        c = by_word.astype(ml_dtypes.float4_e2m1fn).view(np.uint8) & 0xF
        words = (c[..., 0::2] | (c[..., 1::2] << 4)).reshape(k // 512, 128, 2 * n)
    return np.ascontiguousarray(words), np.ascontiguousarray(byte.astype(np.uint8).reshape(k // 512, 16, n))


def unpack_weight(words, scales, fmt):
    g, _, n = scales.shape
    words = np.ascontiguousarray(words).reshape(g, 128, n, -1)
    if fmt == "e4m3":
        vals = words.view(ml_dtypes.float8_e4m3fn).astype(np.float64)
    else:
        nib = np.empty((g, 128, n, 4), np.uint8)
        nib[..., 0::2] = words & 0xF
        nib[..., 1::2] = words >> 4
        vals = E2M1[nib]
    vals = vals * np.repeat(np.exp2(scales.astype(np.float64) - 127.0), 8, axis=1)[..., None]
    return vals.transpose(0, 1, 3, 2).reshape(g * 512, n)


K, T, I, F, M = 512, 2048, 512, 512, 128


def setup_inputs():
    n = np.random.standard_normal
    idx = np.random.permutation(T)[:I]
    fk = mx_kscale(K)
    ff = mx_kscale(F)
    encp = pack_weight(n((K, T)) / fk[:, None], "e2m1")
    return {
        "enc_words": encp[0],
        "enc_scales": encp[1],
        "wk": (n((K, F)) * 1 / np.sqrt(K) * fk[:, None]).astype(np.float32),
        "qterm": (0.5 * n((F, 1))).astype(np.float32),
        "gain": (np.random.uniform(0.5, 2.0, (F, 1)) * ff[:, None]).astype(np.float32),
        "score": (n((F, M)) * 0.8 / np.sqrt(F) / ff[:, None]).astype(np.float32),
        "offs": striped(idx),
    }


def reference(enc_words, enc_scales, wk, qterm, gain, score, offs):
    idx = unstriped(offs)
    encu = unpack_weight(enc_words, enc_scales, "e2m1")
    wkq = mxq(f64(wk), 0, "e4m3")
    encidxg = encu[:, idx]
    z = wkq.T @ encidxg
    h1 = np.tanh(z + f64(qterm)) * f64(gain)
    scoreq = mxq(f64(score), 0, "e4m3")
    h1q = mxq(h1, 0, "e4m3")
    a = scoreq.T @ h1q
    p = np.exp(a - np.max(a, axis=1, keepdims=True))
    y = p / np.sum(p, axis=1, keepdims=True) * 512.0
    return y

@@ -1,0 +1,196 @@
+from contextlib import ExitStack
+
+import concourse.mybir as mybir
+
+K, T, I, F, M = 512, 2048, 512, 512, 128
+FLOPS = 2 * K * F * I + 2 * F * M * I
+
+F32 = mybir.dt.float32
+BF16 = mybir.dt.bfloat16
+I32 = mybir.dt.int32
+U32 = mybir.dt.uint32
+U16 = mybir.dt.uint16
+U8 = mybir.dt.uint8
+FP8X4 = mybir.dt.float8_e4m3fn_x4
+FP4X4 = mybir.dt.float4_e2m1fn_x4
+ACT = mybir.ActivationFunctionType
+ALU = mybir.AluOpType
+
+P = 128
+PACK = 4
+HALF = 256
+CHUNK = 128
+
+
+def tile_attend_additiveattn_kernel(tc, enc_words, enc_scales, wk, qterm, gain, score, offs, out):
+    nc = tc.nc
+    with ExitStack() as ctx:
+        keep = ctx.enter_context(tc.tile_pool(name="keep", bufs=1))
+        zps = ctx.enter_context(tc.psum_pool(name="zps", bufs=6))
+        aps = ctx.enter_context(tc.psum_pool(name="aps", bufs=1))
+
+        offsets = keep.tile([P, I // 16], U16, name="offsets")
+        scale_win = keep.tile([P, T], U8, name="scale_win", align_bytes=64)
+        word_win = keep.tile([P, T], U16, name="word_win", align_bytes=64)
+        wk_raw = keep.tile([P, PACK, F], F32, name="wk_raw", align_bytes=64)
+        score_raw = keep.tile([P, PACK, M], F32, name="score_raw", align_bytes=64)
+        q_col = keep.tile([P, PACK], F32, name="q_col")
+        g_col = keep.tile([P, PACK], F32, name="g_col")
+
+        nc.vector.memset(scale_win[:].bitcast(I32), 0)
+        nc.sync.dma_start(offsets[:], offs)
+        nc.sync.dma_start(out=word_win[:].bitcast(I32), in_=enc_words[0].bitcast(I32))
+        nc.sync.dma_start(out=q_col[:], in_=qterm.rearrange("(p t) o -> p (t o)", t=PACK))
+        for quad in range(4):
+            nc.sync.dma_start(
+                out=scale_win[32 * quad : 32 * quad + 4, :].bitcast(I32),
+                in_=enc_scales[0, 4 * quad : 4 * quad + 4, :].bitcast(I32),
+            )
+        nc.sync.dma_start(out=wk_raw[:], in_=wk.rearrange("(p j) f -> p j f", j=PACK))
+        nc.sync.dma_start(out=score_raw[:], in_=score.rearrange("(p j) m -> p j m", j=PACK))
+        nc.sync.dma_start(out=g_col[:], in_=gain.rearrange("(p t) o -> p (t o)", t=PACK))
+
+        enc_w = keep.tile([P, I], U16, name="enc_w", align_bytes=64)
+        nc.vector.tensor_copy(enc_w[:], word_win[:].indirect(offsets[:]))
+        enc_s = keep.tile([P, I], U8, name="enc_s", align_bytes=64)
+        nc.vector.tensor_copy(enc_s[:], scale_win[:].indirect(offsets[:]))
+
+        wk_dealt = wk_raw[:].rearrange("p j (m u t) -> p u m j t", u=2, t=2)
+        wk_bf0 = keep.tile([P, 2, P, PACK], BF16, name="wk_bf0", align_bytes=64)
+        wk_bf1 = [keep.tile([P, 2, P // 2, PACK], BF16, name="wk_bf1%d" % s, align_bytes=64) for s in range(2)]
+        wk_codes = [keep.tile([P, 2 * P], U32, name="wk_codes%d" % u, align_bytes=64) for u in range(2)]
+        wk_scales = [keep.tile([P, 2 * P], U8, name="wk_scales%d" % u, align_bytes=64) for u in range(2)]
+        nc.vector.tensor_copy(out=wk_bf0[:].rearrange("p t m j -> p m j t"), in_=wk_dealt[:, 0])
+        nc.scalar.copy(out=wk_bf1[0][:].rearrange("p t m j -> p m j t"), in_=wk_dealt[:, 1, 0 : P // 2])
+        nc.vector.tensor_copy(out=wk_bf1[1][:].rearrange("p t m j -> p m j t"), in_=wk_dealt[:, 1, P // 2 : P])
+        for tt in range(2):
+            nc.vector.quantize_mx(
+                out=wk_codes[0][:, tt * P : (tt + 1) * P].bitcast(FP8X4),
+                scales=wk_scales[0][:, tt * P : (tt + 1) * P],
+                in_=wk_bf0[:, tt].rearrange("p m j -> p (m j)"),
+            )
+        for tt in range(2):
+            for s in range(2):
+                cols = slice(tt * P + s * (P // 2), tt * P + (s + 1) * (P // 2))
+                nc.vector.quantize_mx(
+                    out=wk_codes[1][:, cols].bitcast(FP8X4),
+                    scales=wk_scales[1][:, cols],
+                    in_=wk_bf1[s][:, tt].rearrange("p m j -> p (m j)"),
+                )
+
+        score_bf = keep.tile([P, M, PACK], BF16, name="score_bf", tag="wk_bf10", align_bytes=64)
+        score_codes = keep.tile([P, M], U32, name="score_codes", align_bytes=64)
+        score_scales = keep.tile([P, M], U8, name="score_scales", align_bytes=64)
+        nc.vector.tensor_copy(
+            out=score_bf[:].rearrange("p (c i) j -> p c j i", i=2),
+            in_=score_raw[:].rearrange("p j (c i) -> p c j i", i=2),
+        )
+
+        n_chunks = I // CHUNK
+        th = [keep.tile([P, PACK, CHUNK], F32, name="th%d" % c, align_bytes=64) for c in range(n_chunks)]
+        h_bf = [keep.tile([P, CHUNK, PACK], BF16, name="h_bf%d" % c, align_bytes=64) for c in range(n_chunks)]
+        h_codes = [keep.tile([P, CHUNK], U32, name="h_codes%d" % c, align_bytes=64) for c in range(n_chunks)]
+        h_scales = [keep.tile([P, CHUNK], U8, name="h_scales%d" % c, align_bytes=64) for c in range(n_chunks)]
+        g_bc = g_col[:].rearrange("p (a t b) -> p a t b", a=1, b=1).broadcast_to([P, CHUNK // 2, PACK, 2])
+        early = HALF
+        a_early = aps.tile([M, early], F32, name="a_early")
+        a_last = aps.tile([M, I - early], F32, name="a_last")
+
+        z = {}
+
+        def project(first, width):
+            for t in range(PACK):
+                u, tt = divmod(t, 2)
+                bank = zps.tile([P, width], F32, name="z")
+                nc.tensor.matmul_mx(
+                    out=bank[:],
+                    lhsT=wk_codes[u][:, tt * P : (tt + 1) * P].bitcast(FP8X4),
+                    lhsT_scale=wk_scales[u][:, tt * P : (tt + 1) * P],
+                    rhs=enc_w[:, first : first + width].bitcast(FP4X4),
+                    rhs_scale=enc_s[:, first : first + width],
+                    start=True,
+                    stop=True,
+                )
+                for s in range(0, width, CHUNK):
+                    z[((first + s) // CHUNK, t)] = bank[:, s : s + CHUNK]
+
+        def tanh(c):
+            for t in range(PACK):
+                nc.scalar.activation(out=th[c][:, t, :], in_=z[(c, t)], func=ACT.Tanh, bias=q_col[:, t : t + 1], scale=1.0)
+
+        def weigh(c):
+            nc.vector.tensor_tensor(
+                out=h_bf[c][:].rearrange("p (c i) t -> p c t i", i=2),
+                in0=th[c][:].rearrange("p t (c i) -> p c t i", i=2),
+                in1=g_bc,
+                op=ALU.mult,
+            )
+
+        def quantise_and_score(c):
+            nc.vector.quantize_mx(
+                out=h_codes[c][:].bitcast(FP8X4),
+                scales=h_scales[c][:],
+                in_=h_bf[c][:].rearrange("p n t -> p (n t)"),
+            )
+            nc.tensor.matmul_mx(
+                out=(a_early, a_last)[c // 2][:, (c % 2) * CHUNK : (c % 2 + 1) * CHUNK],
+                lhsT=score_codes[:].bitcast(FP8X4),
+                lhsT_scale=score_scales[:],
+                rhs=h_codes[c][:].bitcast(FP8X4),
+                rhs_scale=h_scales[c][:],
+                start=True,
+                stop=True,
+            )
+
+        project(0, CHUNK)
+        tanh(0)
+        project(CHUNK, CHUNK)
+        tanh(1)
+        project(HALF, HALF)
+        tanh(2)
+        tanh(3)
+        weigh(0)
+        nc.vector.quantize_mx(
+            out=score_codes[:].bitcast(FP8X4),
+            scales=score_scales[:],
+            in_=score_bf[:].rearrange("p m j -> p (m j)"),
+        )
+        for c in range(1, n_chunks):
+            weigh(c)
+            quantise_and_score(c - 1)
+        quantise_and_score(n_chunks - 1)
+
+        neg_max_early = keep.tile([M, 1], F32, name="neg_max_early")
+        neg_max = keep.tile([M, 1], F32, name="neg_max")
+        row_sum = keep.tile([M, 1], F32, name="row_sum")
+        inv_sum = keep.tile([M, 1], F32, name="inv_sum")
+        neg_a = keep.tile([M, I], F32, name="neg_a", align_bytes=64)
+        p_sb = keep.tile([M, I], F32, name="p_sb", align_bytes=64)
+
+        nc.vector.tensor_scalar(
+            out=neg_a[:, :early],
+            in0=a_early[:],
+            scalar1=-1.0,
+            scalar2=None,
+            op0=ALU.mult,
+            op1=ALU.min,
+            accum_out=neg_max_early[:],
+        )
+        nc.vector.tensor_scalar(
+            out=neg_a[:, early:],
+            in0=a_last[:],
+            scalar1=-1.0,
+            scalar2=neg_max_early[:],
+            op0=ALU.mult,
+            op1=ALU.min,
+            accum_out=neg_max[:],
+        )
+        nc.scalar.activation(out=p_sb[:], in_=neg_a[:], func=ACT.Exp, bias=neg_max[:], scale=-1.0, accum_out=row_sum[:])
+        nc.vector.reciprocal(out=inv_sum[:], in_=row_sum[:])
+        for h, queue in enumerate((nc.scalar, nc.sync)):
+            cols = slice(h * HALF, (h + 1) * HALF)
+            y_sb = keep.tile([M, HALF], F32, name="y_sb%d" % h, align_bytes=64)
+            nc.vector.tensor_scalar(
+                out=y_sb[:], in0=p_sb[:, cols], scalar1=inv_sum[:], scalar2=float(I), op0=ALU.mult, op1=ALU.mult
+            )
+            queue.dma_start(out=out[:, cols], in_=y_sb[:])

@@ -38,15 +38,15 @@ def tile_attend_additiveattn_kernel(tc, enc_words, enc_scales, wk, qterm, gain, 
         g_col = keep.tile([P, PACK], F32, name="g_col")
 
         nc.vector.memset(scale_win[:].bitcast(I32), 0)
+        words_hbm = enc_words[0].bitcast(I32)
+        words_sb = word_win[:].bitcast(I32)
+        nc.sync.dma_start(out=words_sb[:, : T // 4], in_=words_hbm[:, : T // 4])
         nc.sync.dma_start(offsets[:], offs)
-        nc.sync.dma_start(out=word_win[:].bitcast(I32), in_=enc_words[0].bitcast(I32))
-        nc.sync.dma_start(out=q_col[:], in_=qterm.rearrange("(p t) o -> p (t o)", t=PACK))
-        for quad in range(4):
-            nc.sync.dma_start(
-                out=scale_win[32 * quad : 32 * quad + 4, :].bitcast(I32),
-                in_=enc_scales[0, 4 * quad : 4 * quad + 4, :].bitcast(I32),
-            )
+        nc.sync.dma_start(out=words_sb[:, T // 4 :], in_=words_hbm[:, T // 4 :])
+        for r in range(4):
+            nc.sync.dma_start(out=scale_win[r:P:32, :].bitcast(I32), in_=enc_scales[0, r:16:4, :].bitcast(I32))
         nc.sync.dma_start(out=wk_raw[:], in_=wk.rearrange("(p j) f -> p j f", j=PACK))
+        nc.sync.dma_start(out=q_col[:], in_=qterm.rearrange("(p t) o -> p (t o)", t=PACK))
         nc.sync.dma_start(out=score_raw[:], in_=score.rearrange("(p j) m -> p j m", j=PACK))
         nc.sync.dma_start(out=g_col[:], in_=gain.rearrange("(p t) o -> p (t o)", t=PACK))
 

@@ -18,16 +18,21 @@ ALU = mybir.AluOpType
 
 P = 128
 PACK = 4
-HALF = 256
+QUADRANT = 32
+HALF = I // 2
 CHUNK = 128
+N_CHUNKS = I // CHUNK
 
 
 def tile_attend_additiveattn_kernel(tc, enc_words, enc_scales, wk, qterm, gain, score, offs, out):
     nc = tc.nc
     with ExitStack() as ctx:
         keep = ctx.enter_context(tc.tile_pool(name="keep", bufs=1))
-        zps = ctx.enter_context(tc.psum_pool(name="zps", bufs=6))
+        zps = ctx.enter_context(tc.psum_pool(name="zps", bufs=1))
         aps = ctx.enter_context(tc.psum_pool(name="aps", bufs=1))
+
+        def quantise(codes, scales, values):
+            nc.vector.quantize_mx(out=codes.bitcast(FP8X4), scales=scales, in_=values)
 
         offsets = keep.tile([P, I // 16], U16, name="offsets")
         scale_win = keep.tile([P, T], U8, name="scale_win", align_bytes=64)
@@ -44,7 +49,9 @@ def tile_attend_additiveattn_kernel(tc, enc_words, enc_scales, wk, qterm, gain, 
         nc.sync.dma_start(offsets[:], offs)
         nc.sync.dma_start(out=words_sb[:, T // 4 :], in_=words_hbm[:, T // 4 :])
         for r in range(4):
-            nc.sync.dma_start(out=scale_win[r:P:32, :].bitcast(I32), in_=enc_scales[0, r:16:4, :].bitcast(I32))
+            nc.sync.dma_start(
+                out=scale_win[r:P:QUADRANT, :].bitcast(I32), in_=enc_scales[0, r:16:4, :].bitcast(I32)
+            )
         nc.sync.dma_start(out=wk_raw[:], in_=wk.rearrange("(p j) f -> p j f", j=PACK))
         nc.sync.dma_start(out=q_col[:], in_=qterm.rearrange("(p t) o -> p (t o)", t=PACK))
         nc.sync.dma_start(out=score_raw[:], in_=score.rearrange("(p j) m -> p j m", j=PACK))
@@ -55,83 +62,71 @@ def tile_attend_additiveattn_kernel(tc, enc_words, enc_scales, wk, qterm, gain, 
         enc_s = keep.tile([P, I], U8, name="enc_s", align_bytes=64)
         nc.vector.tensor_copy(enc_s[:], scale_win[:].indirect(offsets[:]))
 
-        wk_dealt = wk_raw[:].rearrange("p j (m u t) -> p u m j t", u=2, t=2)
+        wk_dealt = wk_raw[:].rearrange("p j (m u v) -> p u m j v", u=2, v=2)
         wk_bf0 = keep.tile([P, 2, P, PACK], BF16, name="wk_bf0", align_bytes=64)
         wk_bf1 = [keep.tile([P, 2, P // 2, PACK], BF16, name="wk_bf1%d" % s, align_bytes=64) for s in range(2)]
         wk_codes = [keep.tile([P, 2 * P], U32, name="wk_codes%d" % u, align_bytes=64) for u in range(2)]
         wk_scales = [keep.tile([P, 2 * P], U8, name="wk_scales%d" % u, align_bytes=64) for u in range(2)]
-        nc.vector.tensor_copy(out=wk_bf0[:].rearrange("p t m j -> p m j t"), in_=wk_dealt[:, 0])
-        nc.scalar.copy(out=wk_bf1[0][:].rearrange("p t m j -> p m j t"), in_=wk_dealt[:, 1, 0 : P // 2])
-        nc.vector.tensor_copy(out=wk_bf1[1][:].rearrange("p t m j -> p m j t"), in_=wk_dealt[:, 1, P // 2 : P])
-        for tt in range(2):
-            nc.vector.quantize_mx(
-                out=wk_codes[0][:, tt * P : (tt + 1) * P].bitcast(FP8X4),
-                scales=wk_scales[0][:, tt * P : (tt + 1) * P],
-                in_=wk_bf0[:, tt].rearrange("p m j -> p (m j)"),
-            )
-        for tt in range(2):
+        nc.vector.tensor_copy(out=wk_bf0[:].rearrange("p v m j -> p m j v"), in_=wk_dealt[:, 0])
+        nc.scalar.copy(out=wk_bf1[0][:].rearrange("p v m j -> p m j v"), in_=wk_dealt[:, 1, 0 : P // 2])
+        nc.vector.tensor_copy(out=wk_bf1[1][:].rearrange("p v m j -> p m j v"), in_=wk_dealt[:, 1, P // 2 : P])
+        for v in range(2):
+            cols = slice(v * P, (v + 1) * P)
+            quantise(wk_codes[0][:, cols], wk_scales[0][:, cols], wk_bf0[:, v].rearrange("p m j -> p (m j)"))
+        for v in range(2):
             for s in range(2):
-                cols = slice(tt * P + s * (P // 2), tt * P + (s + 1) * (P // 2))
-                nc.vector.quantize_mx(
-                    out=wk_codes[1][:, cols].bitcast(FP8X4),
-                    scales=wk_scales[1][:, cols],
-                    in_=wk_bf1[s][:, tt].rearrange("p m j -> p (m j)"),
-                )
+                cols = slice(v * P + s * (P // 2), v * P + (s + 1) * (P // 2))
+                quantise(wk_codes[1][:, cols], wk_scales[1][:, cols], wk_bf1[s][:, v].rearrange("p m j -> p (m j)"))
 
         score_bf = keep.tile([P, M, PACK], BF16, name="score_bf", tag="wk_bf10", align_bytes=64)
         score_codes = keep.tile([P, M], U32, name="score_codes", align_bytes=64)
         score_scales = keep.tile([P, M], U8, name="score_scales", align_bytes=64)
         nc.vector.tensor_copy(
-            out=score_bf[:].rearrange("p (c i) j -> p c j i", i=2),
-            in_=score_raw[:].rearrange("p j (c i) -> p c j i", i=2),
+            out=score_bf[:].rearrange("p (n e) j -> p n j e", e=2),
+            in_=score_raw[:].rearrange("p j (n e) -> p n j e", e=2),
         )
 
-        n_chunks = I // CHUNK
-        th = [keep.tile([P, PACK, CHUNK], F32, name="th%d" % c, align_bytes=64) for c in range(n_chunks)]
-        h_bf = [keep.tile([P, CHUNK, PACK], BF16, name="h_bf%d" % c, align_bytes=64) for c in range(n_chunks)]
-        h_codes = [keep.tile([P, CHUNK], U32, name="h_codes%d" % c, align_bytes=64) for c in range(n_chunks)]
-        h_scales = [keep.tile([P, CHUNK], U8, name="h_scales%d" % c, align_bytes=64) for c in range(n_chunks)]
+        th = [keep.tile([P, PACK, CHUNK], F32, name="th%d" % c, align_bytes=64) for c in range(N_CHUNKS)]
+        h_bf = [keep.tile([P, CHUNK, PACK], BF16, name="h_bf%d" % c, align_bytes=64) for c in range(N_CHUNKS)]
+        h_codes = [keep.tile([P, CHUNK], U32, name="h_codes%d" % c, align_bytes=64) for c in range(N_CHUNKS)]
+        h_scales = [keep.tile([P, CHUNK], U8, name="h_scales%d" % c, align_bytes=64) for c in range(N_CHUNKS)]
         g_bc = g_col[:].rearrange("p (a t b) -> p a t b", a=1, b=1).broadcast_to([P, CHUNK // 2, PACK, 2])
-        early = HALF
-        a_early = aps.tile([M, early], F32, name="a_early")
-        a_last = aps.tile([M, I - early], F32, name="a_last")
+        a_early = aps.tile([M, HALF], F32, name="a_early")
+        a_last = aps.tile([M, HALF], F32, name="a_last")
 
         z = {}
 
-        def project(first, width):
+        def project(first, width, outs):
             for t in range(PACK):
-                u, tt = divmod(t, 2)
-                bank = zps.tile([P, width], F32, name="z")
+                u, v = divmod(t, 2)
                 nc.tensor.matmul_mx(
-                    out=bank[:],
-                    lhsT=wk_codes[u][:, tt * P : (tt + 1) * P].bitcast(FP8X4),
-                    lhsT_scale=wk_scales[u][:, tt * P : (tt + 1) * P],
+                    out=outs[t],
+                    lhsT=wk_codes[u][:, v * P : (v + 1) * P].bitcast(FP8X4),
+                    lhsT_scale=wk_scales[u][:, v * P : (v + 1) * P],
                     rhs=enc_w[:, first : first + width].bitcast(FP4X4),
                     rhs_scale=enc_s[:, first : first + width],
                     start=True,
                     stop=True,
                 )
-                for s in range(0, width, CHUNK):
-                    z[((first + s) // CHUNK, t)] = bank[:, s : s + CHUNK]
+                for lo in range(0, width, CHUNK):
+                    z[((first + lo) // CHUNK, t)] = outs[t][:, lo : lo + CHUNK]
 
         def tanh(c):
             for t in range(PACK):
-                nc.scalar.activation(out=th[c][:, t, :], in_=z[(c, t)], func=ACT.Tanh, bias=q_col[:, t : t + 1], scale=1.0)
+                nc.scalar.activation(
+                    out=th[c][:, t, :], in_=z[(c, t)], func=ACT.Tanh, bias=q_col[:, t : t + 1], scale=1.0
+                )
 
         def weigh(c):
             nc.vector.tensor_tensor(
-                out=h_bf[c][:].rearrange("p (c i) t -> p c t i", i=2),
-                in0=th[c][:].rearrange("p t (c i) -> p c t i", i=2),
+                out=h_bf[c][:].rearrange("p (n e) t -> p n t e", e=2),
+                in0=th[c][:].rearrange("p t (n e) -> p n t e", e=2),
                 in1=g_bc,
                 op=ALU.mult,
             )
 
         def quantise_and_score(c):
-            nc.vector.quantize_mx(
-                out=h_codes[c][:].bitcast(FP8X4),
-                scales=h_scales[c][:],
-                in_=h_bf[c][:].rearrange("p n t -> p (n t)"),
-            )
+            quantise(h_codes[c][:], h_scales[c][:], h_bf[c][:].rearrange("p n t -> p (n t)"))
             nc.tensor.matmul_mx(
                 out=(a_early, a_last)[c // 2][:, (c % 2) * CHUNK : (c % 2 + 1) * CHUNK],
                 lhsT=score_codes[:].bitcast(FP8X4),
@@ -142,23 +137,20 @@ def tile_attend_additiveattn_kernel(tc, enc_words, enc_scales, wk, qterm, gain, 
                 stop=True,
             )
 
-        project(0, CHUNK)
+        project(0, CHUNK, [zps.tile([P, CHUNK], F32, name="z_own%d" % t)[:] for t in range(PACK)])
         tanh(0)
-        project(CHUNK, CHUNK)
+        shared = [zps.tile([P, 2, CHUNK], F32, name="z_pair%d" % u) for u in range(2)]
+        project(CHUNK, CHUNK, [shared[t // 2][:, t % 2, :] for t in range(PACK)])
         tanh(1)
-        project(HALF, HALF)
+        project(HALF, HALF, [zps.tile([P, HALF], F32, name="z_own%d" % t)[:] for t in range(PACK)])
         tanh(2)
         tanh(3)
         weigh(0)
-        nc.vector.quantize_mx(
-            out=score_codes[:].bitcast(FP8X4),
-            scales=score_scales[:],
-            in_=score_bf[:].rearrange("p m j -> p (m j)"),
-        )
-        for c in range(1, n_chunks):
+        quantise(score_codes[:], score_scales[:], score_bf[:].rearrange("p m j -> p (m j)"))
+        for c in range(1, N_CHUNKS):
             weigh(c)
             quantise_and_score(c - 1)
-        quantise_and_score(n_chunks - 1)
+        quantise_and_score(N_CHUNKS - 1)
 
         neg_max_early = keep.tile([M, 1], F32, name="neg_max_early")
         neg_max = keep.tile([M, 1], F32, name="neg_max")
@@ -168,7 +160,7 @@ def tile_attend_additiveattn_kernel(tc, enc_words, enc_scales, wk, qterm, gain, 
         p_sb = keep.tile([M, I], F32, name="p_sb", align_bytes=64)
 
         nc.vector.tensor_scalar(
-            out=neg_a[:, :early],
+            out=neg_a[:, :HALF],
             in0=a_early[:],
             scalar1=-1.0,
             scalar2=None,
@@ -177,7 +169,7 @@ def tile_attend_additiveattn_kernel(tc, enc_words, enc_scales, wk, qterm, gain, 
             accum_out=neg_max_early[:],
         )
         nc.vector.tensor_scalar(
-            out=neg_a[:, early:],
+            out=neg_a[:, HALF:],
             in0=a_last[:],
             scalar1=-1.0,
             scalar2=neg_max_early[:],
@@ -191,6 +183,6 @@ def tile_attend_additiveattn_kernel(tc, enc_words, enc_scales, wk, qterm, gain, 
             cols = slice(h * HALF, (h + 1) * HALF)
             y_sb = keep.tile([M, HALF], F32, name="y_sb%d" % h, align_bytes=64)
             nc.vector.tensor_scalar(
-                out=y_sb[:], in0=p_sb[:, cols], scalar1=inv_sum[:], scalar2=float(I), op0=ALU.mult, op1=ALU.mult
+                out=y_sb[:], in0=p_sb[:, cols], scalar1=inv_sum[:], scalar2=512.0, op0=ALU.mult, op1=ALU.mult
             )
             queue.dma_start(out=out[:, cols], in_=y_sb[:])

@@ -22,12 +22,14 @@ QUADRANT = 32
 HALF = I // 2
 CHUNK = 128
 N_CHUNKS = I // CHUNK
+M_HALF = P // 2
 
 
 def tile_attend_additiveattn_kernel(tc, enc_words, enc_scales, wk, qterm, gain, score, offs, out):
     nc = tc.nc
     with ExitStack() as ctx:
         keep = ctx.enter_context(tc.tile_pool(name="keep", bufs=1))
+        reuse = ctx.enter_context(tc.tile_pool(name="reuse", bufs=1))
         zps = ctx.enter_context(tc.psum_pool(name="zps", bufs=1))
         aps = ctx.enter_context(tc.psum_pool(name="aps", bufs=1))
 
@@ -35,50 +37,68 @@ def tile_attend_additiveattn_kernel(tc, enc_words, enc_scales, wk, qterm, gain, 
             nc.vector.quantize_mx(out=codes.bitcast(FP8X4), scales=scales, in_=values)
 
         offsets = keep.tile([P, I // 16], U16, name="offsets")
-        scale_win = keep.tile([P, T], U8, name="scale_win", align_bytes=64)
-        word_win = keep.tile([P, T], U16, name="word_win", align_bytes=64)
-        wk_raw = keep.tile([P, PACK, F], F32, name="wk_raw", align_bytes=64)
-        score_raw = keep.tile([P, PACK, M], F32, name="score_raw", align_bytes=64)
+        scale_win = reuse.tile([P, T], U8, name="scale_win", align_bytes=64, offset=1024)
+        word_win = keep.tile([P, T], U16, name="word_win", tag="word_win", align_bytes=64)
+        wk_raw = [keep.tile([P, PACK, F // 2], F32, name="wk_raw%d" % h, tag="wk_raw%d" % h, align_bytes=64) for h in range(2)]
         q_col = keep.tile([P, PACK], F32, name="q_col")
         g_col = keep.tile([P, PACK], F32, name="g_col")
 
         nc.vector.memset(scale_win[:].bitcast(I32), 0)
+        enc_s = keep.tile([P, I], U8, name="enc_s", align_bytes=64)
+        nc.vector.memset(enc_s[:].bitcast(I32), 0)
+        wk_rows = wk.rearrange("(p j) f -> p j f", j=PACK)
         words_hbm = enc_words[0].bitcast(I32)
         words_sb = word_win[:].bitcast(I32)
         nc.sync.dma_start(out=words_sb[:, : T // 4], in_=words_hbm[:, : T // 4])
         nc.sync.dma_start(offsets[:], offs)
-        nc.sync.dma_start(out=words_sb[:, T // 4 :], in_=words_hbm[:, T // 4 :])
-        for r in range(4):
-            nc.sync.dma_start(
-                out=scale_win[r:P:QUADRANT, :].bitcast(I32), in_=enc_scales[0, r:16:4, :].bitcast(I32)
-            )
-        nc.sync.dma_start(out=wk_raw[:], in_=wk.rearrange("(p j) f -> p j f", j=PACK))
         nc.sync.dma_start(out=q_col[:], in_=qterm.rearrange("(p t) o -> p (t o)", t=PACK))
-        nc.sync.dma_start(out=score_raw[:], in_=score.rearrange("(p j) m -> p j m", j=PACK))
+        nc.sync.dma_start(out=scale_win[0:P:8, :].bitcast(I32), in_=enc_scales[0].bitcast(I32))
+        nc.sync.dma_start(out=words_sb[:, T // 4 :], in_=words_hbm[:, T // 4 :])
+        for h in range(2):
+            nc.sync.dma_start(out=wk_raw[h][:], in_=wk_rows[:, :, h * F // 2 : (h + 1) * F // 2])
         nc.sync.dma_start(out=g_col[:], in_=gain.rearrange("(p t) o -> p (t o)", t=PACK))
 
-        enc_w = keep.tile([P, I], U16, name="enc_w", align_bytes=64)
-        nc.vector.tensor_copy(enc_w[:], word_win[:].indirect(offsets[:]))
-        enc_s = keep.tile([P, I], U8, name="enc_s", align_bytes=64)
-        nc.vector.tensor_copy(enc_s[:], scale_win[:].indirect(offsets[:]))
+        spread_s = keep.tile([P, I], U8, name="spread_s", align_bytes=64)
+        nc.vector.tensor_copy(spread_s[:], scale_win[:].indirect(offsets[:]))
+        for r in range(4):
+            nc.sync.dma_start(out=enc_s[r:P:QUADRANT, :].bitcast(I32), in_=spread_s[8 * r : P : QUADRANT, :].bitcast(I32))
+        score_raw = reuse.tile([P, PACK, M], F32, name="score_raw", align_bytes=64, offset=2048)
+        nc.sync.dma_start(out=score_raw[:], in_=score.rearrange("(p j) m -> p j m", j=PACK))
 
-        wk_dealt = wk_raw[:].rearrange("p j (m u v) -> p u m j v", u=2, v=2)
-        wk_bf0 = keep.tile([P, 2, P, PACK], BF16, name="wk_bf0", align_bytes=64)
-        wk_bf1 = [keep.tile([P, 2, P // 2, PACK], BF16, name="wk_bf1%d" % s, align_bytes=64) for s in range(2)]
-        wk_codes = [keep.tile([P, 2 * P], U32, name="wk_codes%d" % u, align_bytes=64) for u in range(2)]
-        wk_scales = [keep.tile([P, 2 * P], U8, name="wk_scales%d" % u, align_bytes=64) for u in range(2)]
-        nc.vector.tensor_copy(out=wk_bf0[:].rearrange("p v m j -> p m j v"), in_=wk_dealt[:, 0])
-        nc.scalar.copy(out=wk_bf1[0][:].rearrange("p v m j -> p m j v"), in_=wk_dealt[:, 1, 0 : P // 2])
-        nc.vector.tensor_copy(out=wk_bf1[1][:].rearrange("p v m j -> p m j v"), in_=wk_dealt[:, 1, P // 2 : P])
-        for v in range(2):
-            cols = slice(v * P, (v + 1) * P)
-            quantise(wk_codes[0][:, cols], wk_scales[0][:, cols], wk_bf0[:, v].rearrange("p m j -> p (m j)"))
-        for v in range(2):
-            for s in range(2):
-                cols = slice(v * P + s * (P // 2), v * P + (s + 1) * (P // 2))
-                quantise(wk_codes[1][:, cols], wk_scales[1][:, cols], wk_bf1[s][:, v].rearrange("p m j -> p (m j)"))
+        enc_w = [reuse.tile([P, HALF], U16, name="enc_w0", align_bytes=64, offset=1024)]
+        nc.vector.tensor_copy(enc_w[0][:], word_win[:].indirect(offsets[:, : HALF // 16]))
 
-        score_bf = keep.tile([P, M, PACK], BF16, name="score_bf", tag="wk_bf10", align_bytes=64)
+        wk_codes = [keep.tile([P, P], U32, name="wk_codes%d" % t, align_bytes=64) for t in range(PACK)]
+        wk_scales = [keep.tile([P, P], U8, name="wk_scales%d" % t, align_bytes=64) for t in range(PACK)]
+        wk_bf = [
+            [keep.tile([P, 2, M_HALF, PACK], BF16, name="wk_bf%d%d" % (h, u), tag="wk_bf%d%d" % (h, u), align_bytes=64) for u in range(2)]
+            for h in range(2)
+        ]
+
+        def deal(copy, h, u):
+            copy(
+                out=wk_bf[h][u][:].rearrange("p v m j -> p m j v"),
+                in_=wk_raw[h][:].rearrange("p j (m u v) -> p u m j v", u=2, v=2)[:, u],
+            )
+
+        def quantise_wk(h, u):
+            for v in range(2):
+                cols = slice(h * M_HALF, (h + 1) * M_HALF)
+                t = 2 * u + v
+                quantise(wk_codes[t][:, cols], wk_scales[t][:, cols], wk_bf[h][u][:, v].rearrange("p m j -> p (m j)"))
+
+        deal(nc.scalar.copy, 0, 1)
+        deal(nc.vector.tensor_copy, 0, 0)
+        quantise_wk(0, 1)
+        quantise_wk(0, 0)
+        deal(nc.vector.tensor_copy, 1, 0)
+        deal(nc.scalar.copy, 1, 1)
+        quantise_wk(1, 0)
+        quantise_wk(1, 1)
+        enc_w.append(keep.tile([P, HALF], U16, name="enc_w1", tag="wk_bf11", align_bytes=64))
+        nc.vector.tensor_copy(enc_w[1][:], word_win[:].indirect(offsets[:, HALF // 16 :]))
+
+        score_bf = keep.tile([P, M, PACK], BF16, name="score_bf", tag="word_win", align_bytes=64)
         score_codes = keep.tile([P, M], U32, name="score_codes", align_bytes=64)
         score_scales = keep.tile([P, M], U8, name="score_scales", align_bytes=64)
         nc.vector.tensor_copy(
@@ -94,27 +114,21 @@ def tile_attend_additiveattn_kernel(tc, enc_words, enc_scales, wk, qterm, gain, 
         a_early = aps.tile([M, HALF], F32, name="a_early")
         a_last = aps.tile([M, HALF], F32, name="a_last")
 
-        z = {}
-
-        def project(first, width, outs):
+        def project_and_tanh(c, z):
+            h, lo = divmod(c * CHUNK, HALF)
             for t in range(PACK):
-                u, v = divmod(t, 2)
                 nc.tensor.matmul_mx(
-                    out=outs[t],
-                    lhsT=wk_codes[u][:, v * P : (v + 1) * P].bitcast(FP8X4),
-                    lhsT_scale=wk_scales[u][:, v * P : (v + 1) * P],
-                    rhs=enc_w[:, first : first + width].bitcast(FP4X4),
-                    rhs_scale=enc_s[:, first : first + width],
+                    out=z[t],
+                    lhsT=wk_codes[t][:].bitcast(FP8X4),
+                    lhsT_scale=wk_scales[t][:],
+                    rhs=enc_w[h][:, lo : lo + CHUNK].bitcast(FP4X4),
+                    rhs_scale=enc_s[:, c * CHUNK : (c + 1) * CHUNK],
                     start=True,
                     stop=True,
                 )
-                for lo in range(0, width, CHUNK):
-                    z[((first + lo) // CHUNK, t)] = outs[t][:, lo : lo + CHUNK]
-
-        def tanh(c):
             for t in range(PACK):
                 nc.scalar.activation(
-                    out=th[c][:, t, :], in_=z[(c, t)], func=ACT.Tanh, bias=q_col[:, t : t + 1], scale=1.0
+                    out=th[c][:, t, :], in_=z[t], func=ACT.Tanh, bias=q_col[:, t : t + 1], scale=1.0
                 )
 
         def weigh(c):
@@ -137,14 +151,10 @@ def tile_attend_additiveattn_kernel(tc, enc_words, enc_scales, wk, qterm, gain, 
                 stop=True,
             )
 
-        project(0, CHUNK, [zps.tile([P, CHUNK], F32, name="z_own%d" % t)[:] for t in range(PACK)])
-        tanh(0)
-        shared = [zps.tile([P, 2, CHUNK], F32, name="z_pair%d" % u) for u in range(2)]
-        project(CHUNK, CHUNK, [shared[t // 2][:, t % 2, :] for t in range(PACK)])
-        tanh(1)
-        project(HALF, HALF, [zps.tile([P, HALF], F32, name="z_own%d" % t)[:] for t in range(PACK)])
-        tanh(2)
-        tanh(3)
+        project_and_tanh(0, [zps.tile([P, CHUNK], F32, name="z%d" % t, tag="bank%d" % t)[:] for t in range(PACK)])
+        for c, banks in ((1, (4, 5)), (2, (0, 1)), (3, (2, 3))):
+            pair = [zps.tile([P, 2, CHUNK], F32, name="z_pair%d" % b, tag="bank%d" % b) for b in banks]
+            project_and_tanh(c, [pair[t // 2][:, t % 2, :] for t in range(PACK)])
         weigh(0)
         quantise(score_codes[:], score_scales[:], score_bf[:].rearrange("p m j -> p (m j)"))
         for c in range(1, N_CHUNKS):

@@ -22,6 +22,8 @@ QUADRANT = 32
 HALF = I // 2
 CHUNK = 128
 N_CHUNKS = I // CHUNK
+M_SCALAR = 24
+LEAD = 128
 M_HALF = P // 2
 
 
@@ -49,13 +51,14 @@ def tile_attend_additiveattn_kernel(tc, enc_words, enc_scales, wk, qterm, gain, 
         wk_rows = wk.rearrange("(p j) f -> p j f", j=PACK)
         words_hbm = enc_words[0].bitcast(I32)
         words_sb = word_win[:].bitcast(I32)
-        nc.sync.dma_start(out=words_sb[:, : T // 4], in_=words_hbm[:, : T // 4])
+        nc.sync.dma_start(out=words_sb[:, :LEAD], in_=words_hbm[:, :LEAD])
         nc.sync.dma_start(offsets[:], offs)
-        nc.sync.dma_start(out=q_col[:], in_=qterm.rearrange("(p t) o -> p (t o)", t=PACK))
+        nc.sync.dma_start(out=words_sb[:, LEAD : 2 * LEAD], in_=words_hbm[:, LEAD : 2 * LEAD])
         nc.sync.dma_start(out=scale_win[0:P:8, :].bitcast(I32), in_=enc_scales[0].bitcast(I32))
-        nc.sync.dma_start(out=words_sb[:, T // 4 :], in_=words_hbm[:, T // 4 :])
+        nc.sync.dma_start(out=words_sb[:, 2 * LEAD :], in_=words_hbm[:, 2 * LEAD :])
         for h in range(2):
             nc.sync.dma_start(out=wk_raw[h][:], in_=wk_rows[:, :, h * F // 2 : (h + 1) * F // 2])
+        nc.sync.dma_start(out=q_col[:], in_=qterm.rearrange("(p t) o -> p (t o)", t=PACK))
         nc.sync.dma_start(out=g_col[:], in_=gain.rearrange("(p t) o -> p (t o)", t=PACK))
 
         spread_s = keep.tile([P, I], U8, name="spread_s", align_bytes=64)
@@ -65,20 +68,20 @@ def tile_attend_additiveattn_kernel(tc, enc_words, enc_scales, wk, qterm, gain, 
         score_raw = reuse.tile([P, PACK, M], F32, name="score_raw", align_bytes=64, offset=2048)
         nc.sync.dma_start(out=score_raw[:], in_=score.rearrange("(p j) m -> p j m", j=PACK))
 
-        enc_w = [reuse.tile([P, HALF], U16, name="enc_w0", align_bytes=64, offset=1024)]
+        enc_w = [keep.tile([P, HALF], U16, name="enc_w0", align_bytes=64)]
         nc.vector.tensor_copy(enc_w[0][:], word_win[:].indirect(offsets[:, : HALF // 16]))
 
         wk_codes = [keep.tile([P, P], U32, name="wk_codes%d" % t, align_bytes=64) for t in range(PACK)]
         wk_scales = [keep.tile([P, P], U8, name="wk_scales%d" % t, align_bytes=64) for t in range(PACK)]
         wk_bf = [
-            [keep.tile([P, 2, M_HALF, PACK], BF16, name="wk_bf%d%d" % (h, u), tag="wk_bf%d%d" % (h, u), align_bytes=64) for u in range(2)]
+            [reuse.tile([P, 2, M_HALF, PACK], BF16, name="wk_bf%d%d" % (h, u), align_bytes=64, offset=4096 + 2048 * (2 * h + u)) for u in range(2)]
             for h in range(2)
         ]
 
-        def deal(copy, h, u):
+        def deal(copy, h, u, cols):
             copy(
-                out=wk_bf[h][u][:].rearrange("p v m j -> p m j v"),
-                in_=wk_raw[h][:].rearrange("p j (m u v) -> p u m j v", u=2, v=2)[:, u],
+                out=wk_bf[h][u][:, :, cols, :].rearrange("p v m j -> p m j v"),
+                in_=wk_raw[h][:].rearrange("p j (m u v) -> p u m j v", u=2, v=2)[:, u, cols],
             )
 
         def quantise_wk(h, u):
@@ -87,18 +90,19 @@ def tile_attend_additiveattn_kernel(tc, enc_words, enc_scales, wk, qterm, gain, 
                 t = 2 * u + v
                 quantise(wk_codes[t][:, cols], wk_scales[t][:, cols], wk_bf[h][u][:, v].rearrange("p m j -> p (m j)"))
 
-        deal(nc.scalar.copy, 0, 1)
-        deal(nc.vector.tensor_copy, 0, 0)
-        quantise_wk(0, 1)
+        deal(nc.scalar.copy, 0, 0, slice(0, M_HALF))
+        deal(nc.scalar.copy, 0, 1, slice(0, M_HALF))
         quantise_wk(0, 0)
-        deal(nc.vector.tensor_copy, 1, 0)
-        deal(nc.scalar.copy, 1, 1)
-        quantise_wk(1, 0)
-        quantise_wk(1, 1)
-        enc_w.append(keep.tile([P, HALF], U16, name="enc_w1", tag="wk_bf11", align_bytes=64))
+        quantise_wk(0, 1)
+        for u in range(2):
+            deal(nc.vector.tensor_copy, 1, u, slice(M_SCALAR, M_HALF))
+            deal(nc.scalar.copy, 1, u, slice(0, M_SCALAR))
+        for u in range(2):
+            quantise_wk(1, u)
+        enc_w.append(reuse.tile([P, HALF], U16, name="enc_w1", align_bytes=64, offset=8192))
         nc.vector.tensor_copy(enc_w[1][:], word_win[:].indirect(offsets[:, HALF // 16 :]))
 
-        score_bf = keep.tile([P, M, PACK], BF16, name="score_bf", tag="word_win", align_bytes=64)
+        score_bf = reuse.tile([P, M, PACK], BF16, name="score_bf", align_bytes=64, offset=10240)
         score_codes = keep.tile([P, M], U32, name="score_codes", align_bytes=64)
         score_scales = keep.tile([P, M], U8, name="score_scales", align_bytes=64)
         nc.vector.tensor_copy(

@@ -23,7 +23,7 @@ HALF = I // 2
 CHUNK = 128
 N_CHUNKS = I // CHUNK
 M_SCALAR = 24
-LEAD = 128
+CUT0, CUT1 = 512, 768
 M_HALF = P // 2
 
 
@@ -51,11 +51,11 @@ def tile_attend_additiveattn_kernel(tc, enc_words, enc_scales, wk, qterm, gain, 
         wk_rows = wk.rearrange("(p j) f -> p j f", j=PACK)
         words_hbm = enc_words[0].bitcast(I32)
         words_sb = word_win[:].bitcast(I32)
-        nc.sync.dma_start(out=words_sb[:, :LEAD], in_=words_hbm[:, :LEAD])
+        nc.sync.dma_start(out=words_sb[:, :CUT0], in_=words_hbm[:, :CUT0])
         nc.sync.dma_start(offsets[:], offs)
-        nc.sync.dma_start(out=words_sb[:, LEAD : 2 * LEAD], in_=words_hbm[:, LEAD : 2 * LEAD])
+        nc.sync.dma_start(out=words_sb[:, CUT0:CUT1], in_=words_hbm[:, CUT0:CUT1])
         nc.sync.dma_start(out=scale_win[0:P:8, :].bitcast(I32), in_=enc_scales[0].bitcast(I32))
-        nc.sync.dma_start(out=words_sb[:, 2 * LEAD :], in_=words_hbm[:, 2 * LEAD :])
+        nc.sync.dma_start(out=words_sb[:, CUT1:], in_=words_hbm[:, CUT1:])
         for h in range(2):
             nc.sync.dma_start(out=wk_raw[h][:], in_=wk_rows[:, :, h * F // 2 : (h + 1) * F // 2])
         nc.sync.dma_start(out=q_col[:], in_=qterm.rearrange("(p t) o -> p (t o)", t=PACK))

@@ -22,8 +22,6 @@ QUADRANT = 32
 HALF = I // 2
 CHUNK = 128
 N_CHUNKS = I // CHUNK
-M_SCALAR = 24
-CUT0, CUT1 = 512, 768
 M_HALF = P // 2
 
 
@@ -41,7 +39,7 @@ def tile_attend_additiveattn_kernel(tc, enc_words, enc_scales, wk, qterm, gain, 
         offsets = keep.tile([P, I // 16], U16, name="offsets")
         scale_win = reuse.tile([P, T], U8, name="scale_win", align_bytes=64, offset=1024)
         word_win = keep.tile([P, T], U16, name="word_win", tag="word_win", align_bytes=64)
-        wk_raw = [keep.tile([P, PACK, F // 2], F32, name="wk_raw%d" % h, tag="wk_raw%d" % h, align_bytes=64) for h in range(2)]
+        wk_raw = [keep.tile([P, PACK, w], F32, name="wk_raw%d" % h, align_bytes=64) for h, w in enumerate((F // 4, F // 4, F // 2))]
         q_col = keep.tile([P, PACK], F32, name="q_col")
         g_col = keep.tile([P, PACK], F32, name="g_col")
 
@@ -49,15 +47,15 @@ def tile_attend_additiveattn_kernel(tc, enc_words, enc_scales, wk, qterm, gain, 
         enc_s = keep.tile([P, I], U8, name="enc_s", align_bytes=64)
         nc.vector.memset(enc_s[:].bitcast(I32), 0)
         wk_rows = wk.rearrange("(p j) f -> p j f", j=PACK)
+        nc.sync.dma_start(out=wk_raw[0][:], in_=wk_rows[:, :, : F // 4])
+        nc.sync.dma_start(offsets[:], offs)
         words_hbm = enc_words[0].bitcast(I32)
         words_sb = word_win[:].bitcast(I32)
-        nc.sync.dma_start(out=words_sb[:, :CUT0], in_=words_hbm[:, :CUT0])
-        nc.sync.dma_start(offsets[:], offs)
-        nc.sync.dma_start(out=words_sb[:, CUT0:CUT1], in_=words_hbm[:, CUT0:CUT1])
+        nc.sync.dma_start(out=words_sb[:, : T // 8], in_=words_hbm[:, : T // 8])
         nc.sync.dma_start(out=scale_win[0:P:8, :].bitcast(I32), in_=enc_scales[0].bitcast(I32))
-        nc.sync.dma_start(out=words_sb[:, CUT1:], in_=words_hbm[:, CUT1:])
-        for h in range(2):
-            nc.sync.dma_start(out=wk_raw[h][:], in_=wk_rows[:, :, h * F // 2 : (h + 1) * F // 2])
+        nc.sync.dma_start(out=wk_raw[1][:], in_=wk_rows[:, :, F // 4 : F // 2])
+        nc.sync.dma_start(out=wk_raw[2][:], in_=wk_rows[:, :, F // 2 :])
+        nc.sync.dma_start(out=words_sb[:, T // 8 :], in_=words_hbm[:, T // 8 :])
         nc.sync.dma_start(out=q_col[:], in_=qterm.rearrange("(p t) o -> p (t o)", t=PACK))
         nc.sync.dma_start(out=g_col[:], in_=gain.rearrange("(p t) o -> p (t o)", t=PACK))
 
@@ -68,9 +66,6 @@ def tile_attend_additiveattn_kernel(tc, enc_words, enc_scales, wk, qterm, gain, 
         score_raw = reuse.tile([P, PACK, M], F32, name="score_raw", align_bytes=64, offset=2048)
         nc.sync.dma_start(out=score_raw[:], in_=score.rearrange("(p j) m -> p j m", j=PACK))
 
-        enc_w = [keep.tile([P, HALF], U16, name="enc_w0", align_bytes=64)]
-        nc.vector.tensor_copy(enc_w[0][:], word_win[:].indirect(offsets[:, : HALF // 16]))
-
         wk_codes = [keep.tile([P, P], U32, name="wk_codes%d" % t, align_bytes=64) for t in range(PACK)]
         wk_scales = [keep.tile([P, P], U8, name="wk_scales%d" % t, align_bytes=64) for t in range(PACK)]
         wk_bf = [
@@ -78,10 +73,10 @@ def tile_attend_additiveattn_kernel(tc, enc_words, enc_scales, wk, qterm, gain, 
             for h in range(2)
         ]
 
-        def deal(copy, h, u, cols):
+        def deal(copy, piece, h, u, cols, src_cols):
             copy(
                 out=wk_bf[h][u][:, :, cols, :].rearrange("p v m j -> p m j v"),
-                in_=wk_raw[h][:].rearrange("p j (m u v) -> p u m j v", u=2, v=2)[:, u, cols],
+                in_=wk_raw[piece][:].rearrange("p j (m u v) -> p u m j v", u=2, v=2)[:, u, src_cols],
             )
 
         def quantise_wk(h, u):
@@ -90,19 +85,24 @@ def tile_attend_additiveattn_kernel(tc, enc_words, enc_scales, wk, qterm, gain, 
                 t = 2 * u + v
                 quantise(wk_codes[t][:, cols], wk_scales[t][:, cols], wk_bf[h][u][:, v].rearrange("p m j -> p (m j)"))
 
-        deal(nc.scalar.copy, 0, 0, slice(0, M_HALF))
-        deal(nc.scalar.copy, 0, 1, slice(0, M_HALF))
+        low, high, whole = slice(0, M_HALF // 2), slice(M_HALF // 2, M_HALF), slice(0, M_HALF)
+        for piece, cols in enumerate((low, high)):
+            for u in range(2):
+                deal(nc.scalar.copy, piece, 0, u, cols, low)
+        deal(nc.scalar.copy, 2, 1, 0, low, low)
+        deal(nc.scalar.copy, 2, 1, 1, whole, whole)
         quantise_wk(0, 0)
         quantise_wk(0, 1)
-        for u in range(2):
-            deal(nc.vector.tensor_copy, 1, u, slice(M_SCALAR, M_HALF))
-            deal(nc.scalar.copy, 1, u, slice(0, M_SCALAR))
-        for u in range(2):
-            quantise_wk(1, u)
-        enc_w.append(reuse.tile([P, HALF], U16, name="enc_w1", align_bytes=64, offset=8192))
+        deal(nc.vector.tensor_copy, 2, 1, 0, high, high)
+        quantise_wk(1, 0)
+        enc_w = [keep.tile([P, HALF], U16, name="enc_w0", align_bytes=64)]
+        nc.vector.tensor_copy(enc_w[0][:], word_win[:].indirect(offsets[:, : HALF // 16]))
+
+        quantise_wk(1, 1)
+        enc_w.append(reuse.tile([P, HALF], U16, name="enc_w1", align_bytes=64, offset=10240))
         nc.vector.tensor_copy(enc_w[1][:], word_win[:].indirect(offsets[:, HALF // 16 :]))
 
-        score_bf = reuse.tile([P, M, PACK], BF16, name="score_bf", align_bytes=64, offset=10240)
+        score_bf = reuse.tile([P, M, PACK], BF16, name="score_bf", align_bytes=64, offset=10752)
         score_codes = keep.tile([P, M], U32, name="score_codes", align_bytes=64)
         score_scales = keep.tile([P, M], U8, name="score_scales", align_bytes=64)
         nc.vector.tensor_copy(
@@ -111,7 +111,7 @@ def tile_attend_additiveattn_kernel(tc, enc_words, enc_scales, wk, qterm, gain, 
         )
 
         th = [keep.tile([P, PACK, CHUNK], F32, name="th%d" % c, align_bytes=64) for c in range(N_CHUNKS)]
-        h_bf = [keep.tile([P, CHUNK, PACK], BF16, name="h_bf%d" % c, align_bytes=64) for c in range(N_CHUNKS)]
+        h_bf = [keep.tile([P, CHUNK, PACK], BF16, name="h_bf%d" % c, tag="h_bf%d" % c, align_bytes=64) for c in range(N_CHUNKS)]
         h_codes = [keep.tile([P, CHUNK], U32, name="h_codes%d" % c, align_bytes=64) for c in range(N_CHUNKS)]
         h_scales = [keep.tile([P, CHUNK], U8, name="h_scales%d" % c, align_bytes=64) for c in range(N_CHUNKS)]
         g_bc = g_col[:].rearrange("p (a t b) -> p a t b", a=1, b=1).broadcast_to([P, CHUNK // 2, PACK, 2])
@@ -170,7 +170,7 @@ def tile_attend_additiveattn_kernel(tc, enc_words, enc_scales, wk, qterm, gain, 
         neg_max = keep.tile([M, 1], F32, name="neg_max")
         row_sum = keep.tile([M, 1], F32, name="row_sum")
         inv_sum = keep.tile([M, 1], F32, name="inv_sum")
-        neg_a = keep.tile([M, I], F32, name="neg_a", align_bytes=64)
+        neg_a = keep.tile([M, I], F32, name="neg_a", tag="h_bf2", align_bytes=64)
         p_sb = keep.tile([M, I], F32, name="p_sb", align_bytes=64)
 
         nc.vector.tensor_scalar(

@@ -22,6 +22,7 @@ QUADRANT = 32
 HALF = I // 2
 CHUNK = 128
 N_CHUNKS = I // CHUNK
+M_SCALAR = 24
 M_HALF = P // 2
 
 
@@ -85,20 +86,22 @@ def tile_attend_additiveattn_kernel(tc, enc_words, enc_scales, wk, qterm, gain, 
                 t = 2 * u + v
                 quantise(wk_codes[t][:, cols], wk_scales[t][:, cols], wk_bf[h][u][:, v].rearrange("p m j -> p (m j)"))
 
-        low, high, whole = slice(0, M_HALF // 2), slice(M_HALF // 2, M_HALF), slice(0, M_HALF)
+        low, high = slice(0, M_HALF // 2), slice(M_HALF // 2, M_HALF)
         for piece, cols in enumerate((low, high)):
             for u in range(2):
                 deal(nc.scalar.copy, piece, 0, u, cols, low)
-        deal(nc.scalar.copy, 2, 1, 0, low, low)
-        deal(nc.scalar.copy, 2, 1, 1, whole, whole)
+        by_scalar, by_vector = slice(0, M_SCALAR), slice(M_SCALAR, M_HALF)
+        for u in range(2):
+            deal(nc.scalar.copy, 2, 1, u, by_scalar, by_scalar)
         quantise_wk(0, 0)
         quantise_wk(0, 1)
-        deal(nc.vector.tensor_copy, 2, 1, 0, high, high)
+        for u in range(2):
+            deal(nc.vector.tensor_copy, 2, 1, u, by_vector, by_vector)
         quantise_wk(1, 0)
+        quantise_wk(1, 1)
         enc_w = [keep.tile([P, HALF], U16, name="enc_w0", align_bytes=64)]
         nc.vector.tensor_copy(enc_w[0][:], word_win[:].indirect(offsets[:, : HALF // 16]))
 
-        quantise_wk(1, 1)
         enc_w.append(reuse.tile([P, HALF], U16, name="enc_w1", align_bytes=64, offset=10240))
         nc.vector.tensor_copy(enc_w[1][:], word_win[:].indirect(offsets[:, HALF // 16 :]))
 

@@ -138,22 +138,22 @@ def tile_attend_additiveattn_kernel(tc, enc_words, enc_scales, wk, qterm, gain, 
                     out=th[c][:, t, :], in_=z[t], func=ACT.Tanh, bias=q_col[:, t : t + 1], scale=1.0
                 )
 
-        def weigh(c):
+        def weigh(c, lo=0, hi=CHUNK):
             nc.vector.tensor_tensor(
-                out=h_bf[c][:].rearrange("p (n e) t -> p n t e", e=2),
-                in0=th[c][:].rearrange("p t (n e) -> p n t e", e=2),
-                in1=g_bc,
+                out=h_bf[c][:, lo:hi].rearrange("p (n e) t -> p n t e", e=2),
+                in0=th[c][:, :, lo:hi].rearrange("p t (n e) -> p n t e", e=2),
+                in1=g_bc[:, : (hi - lo) // 2],
                 op=ALU.mult,
             )
 
-        def quantise_and_score(c):
-            quantise(h_codes[c][:], h_scales[c][:], h_bf[c][:].rearrange("p n t -> p (n t)"))
+        def quantise_and_score(c, lo=0, hi=CHUNK):
+            quantise(h_codes[c][:, lo:hi], h_scales[c][:, lo:hi], h_bf[c][:, lo:hi].rearrange("p n t -> p (n t)"))
             nc.tensor.matmul_mx(
-                out=(a_early, a_last)[c // 2][:, (c % 2) * CHUNK : (c % 2 + 1) * CHUNK],
+                out=(a_early, a_last)[c // 2][:, (c % 2) * CHUNK + lo : (c % 2) * CHUNK + hi],
                 lhsT=score_codes[:].bitcast(FP8X4),
                 lhsT_scale=score_scales[:],
-                rhs=h_codes[c][:].bitcast(FP8X4),
-                rhs_scale=h_scales[c][:],
+                rhs=h_codes[c][:, lo:hi].bitcast(FP8X4),
+                rhs_scale=h_scales[c][:, lo:hi],
                 start=True,
                 stop=True,
             )
@@ -164,10 +164,15 @@ def tile_attend_additiveattn_kernel(tc, enc_words, enc_scales, wk, qterm, gain, 
             project_and_tanh(c, [pair[t // 2][:, t % 2, :] for t in range(PACK)])
         weigh(0)
         quantise(score_codes[:], score_scales[:], score_bf[:].rearrange("p m j -> p (m j)"))
-        for c in range(1, N_CHUNKS):
+        last = N_CHUNKS - 1
+        for c in range(1, last):
             weigh(c)
             quantise_and_score(c - 1)
-        quantise_and_score(N_CHUNKS - 1)
+        weigh(last, 0, CHUNK // 2)
+        weigh(last, CHUNK // 2, CHUNK)
+        quantise_and_score(last - 1)
+        quantise_and_score(last, 0, CHUNK // 2)
+        quantise_and_score(last, CHUNK // 2, CHUNK)
 
         neg_max_early = keep.tile([M, 1], F32, name="neg_max_early")
         neg_max = keep.tile([M, 1], F32, name="neg_max")

@@ -52,11 +52,10 @@ def tile_attend_additiveattn_kernel(tc, enc_words, enc_scales, wk, qterm, gain, 
         nc.sync.dma_start(offsets[:], offs)
         words_hbm = enc_words[0].bitcast(I32)
         words_sb = word_win[:].bitcast(I32)
-        nc.sync.dma_start(out=words_sb[:, : T // 8], in_=words_hbm[:, : T // 8])
         nc.sync.dma_start(out=scale_win[0:P:8, :].bitcast(I32), in_=enc_scales[0].bitcast(I32))
         nc.sync.dma_start(out=wk_raw[1][:], in_=wk_rows[:, :, F // 4 : F // 2])
         nc.sync.dma_start(out=wk_raw[2][:], in_=wk_rows[:, :, F // 2 :])
-        nc.sync.dma_start(out=words_sb[:, T // 8 :], in_=words_hbm[:, T // 8 :])
+        nc.sync.dma_start(out=words_sb, in_=words_hbm)
         nc.sync.dma_start(out=q_col[:], in_=qterm.rearrange("(p t) o -> p (t o)", t=PACK))
         nc.sync.dma_start(out=g_col[:], in_=gain.rearrange("(p t) o -> p (t o)", t=PACK))
 
@@ -201,9 +200,9 @@ def tile_attend_additiveattn_kernel(tc, enc_words, enc_scales, wk, qterm, gain, 
         )
         nc.scalar.activation(out=p_sb[:], in_=neg_a[:], func=ACT.Exp, bias=neg_max[:], scale=-1.0, accum_out=row_sum[:])
         nc.vector.reciprocal(out=inv_sum[:], in_=row_sum[:])
-        for h, queue in enumerate((nc.scalar, nc.sync)):
-            cols = slice(h * HALF, (h + 1) * HALF)
-            y_sb = keep.tile([M, HALF], F32, name="y_sb%d" % h, align_bytes=64)
+        for h, (queue, lo, hi) in enumerate(((nc.sync, 0, 128), (nc.scalar, 128, 320), (nc.sync, 320, I))):
+            cols = slice(lo, hi)
+            y_sb = keep.tile([M, hi - lo], F32, name="y_sb%d" % h, align_bytes=64)
             nc.vector.tensor_scalar(
                 out=y_sb[:], in0=p_sb[:, cols], scalar1=inv_sum[:], scalar2=512.0, op0=ALU.mult, op1=ALU.mult
             )

@@ -22,8 +22,7 @@ QUADRANT = 32
 HALF = I // 2
 CHUNK = 128
 N_CHUNKS = I // CHUNK
-M_SCALAR = 24
-M_HALF = P // 2
+M_SCALAR = (42, 96)
 
 
 def tile_attend_additiveattn_kernel(tc, enc_words, enc_scales, wk, qterm, gain, score, offs, out):
@@ -38,24 +37,22 @@ def tile_attend_additiveattn_kernel(tc, enc_words, enc_scales, wk, qterm, gain, 
             nc.vector.quantize_mx(out=codes.bitcast(FP8X4), scales=scales, in_=values)
 
         offsets = keep.tile([P, I // 16], U16, name="offsets")
-        scale_win = reuse.tile([P, T], U8, name="scale_win", align_bytes=64, offset=1024)
-        word_win = keep.tile([P, T], U16, name="word_win", tag="word_win", align_bytes=64)
-        wk_raw = [keep.tile([P, PACK, w], F32, name="wk_raw%d" % h, align_bytes=64) for h, w in enumerate((F // 4, F // 4, F // 2))]
+        scale_win = reuse.tile([P, T], U8, name="scale_win", align_bytes=64, offset=0)
+        word_win = keep.tile([P, T], U16, name="word_win", align_bytes=64)
+        wk_raw = keep.tile([P, PACK, F], F32, name="wk_raw", align_bytes=64)
         q_col = keep.tile([P, PACK], F32, name="q_col")
         g_col = keep.tile([P, PACK], F32, name="g_col")
+        enc_s = keep.tile([P, I], U8, name="enc_s", align_bytes=64)
 
         nc.vector.memset(scale_win[:].bitcast(I32), 0)
-        enc_s = keep.tile([P, I], U8, name="enc_s", align_bytes=64)
         nc.vector.memset(enc_s[:].bitcast(I32), 0)
         wk_rows = wk.rearrange("(p j) f -> p j f", j=PACK)
-        nc.sync.dma_start(out=wk_raw[0][:], in_=wk_rows[:, :, : F // 4])
+        nc.sync.dma_start(out=wk_raw[:, :1], in_=wk_rows[:, :1])
         nc.sync.dma_start(offsets[:], offs)
-        words_hbm = enc_words[0].bitcast(I32)
-        words_sb = word_win[:].bitcast(I32)
         nc.sync.dma_start(out=scale_win[0:P:8, :].bitcast(I32), in_=enc_scales[0].bitcast(I32))
-        nc.sync.dma_start(out=wk_raw[1][:], in_=wk_rows[:, :, F // 4 : F // 2])
-        nc.sync.dma_start(out=wk_raw[2][:], in_=wk_rows[:, :, F // 2 :])
-        nc.sync.dma_start(out=words_sb, in_=words_hbm)
+        nc.sync.dma_start(out=wk_raw[:, 1:2], in_=wk_rows[:, 1:2])
+        nc.sync.dma_start(out=wk_raw[:, 2:], in_=wk_rows[:, 2:])
+        nc.sync.dma_start(out=word_win[:].bitcast(I32), in_=enc_words[0].bitcast(I32))
         nc.sync.dma_start(out=q_col[:], in_=qterm.rearrange("(p t) o -> p (t o)", t=PACK))
         nc.sync.dma_start(out=g_col[:], in_=gain.rearrange("(p t) o -> p (t o)", t=PACK))
 
@@ -63,48 +60,38 @@ def tile_attend_additiveattn_kernel(tc, enc_words, enc_scales, wk, qterm, gain, 
         nc.vector.tensor_copy(spread_s[:], scale_win[:].indirect(offsets[:]))
         for r in range(4):
             nc.sync.dma_start(out=enc_s[r:P:QUADRANT, :].bitcast(I32), in_=spread_s[8 * r : P : QUADRANT, :].bitcast(I32))
-        score_raw = reuse.tile([P, PACK, M], F32, name="score_raw", align_bytes=64, offset=2048)
+        score_raw = reuse.tile([P, PACK, M], F32, name="score_raw", align_bytes=64, offset=0)
         nc.sync.dma_start(out=score_raw[:], in_=score.rearrange("(p j) m -> p j m", j=PACK))
 
         wk_codes = [keep.tile([P, P], U32, name="wk_codes%d" % t, align_bytes=64) for t in range(PACK)]
         wk_scales = [keep.tile([P, P], U8, name="wk_scales%d" % t, align_bytes=64) for t in range(PACK)]
-        wk_bf = [
-            [reuse.tile([P, 2, M_HALF, PACK], BF16, name="wk_bf%d%d" % (h, u), align_bytes=64, offset=4096 + 2048 * (2 * h + u)) for u in range(2)]
-            for h in range(2)
-        ]
+        wk_bf = [reuse.tile([P, 2, P, PACK], BF16, name="wk_bf%d" % u, align_bytes=64, offset=2048 * (1 + u)) for u in range(2)]
 
-        def deal(copy, piece, h, u, cols, src_cols):
+        def deal(copy, u, cols, places=slice(0, PACK)):
             copy(
-                out=wk_bf[h][u][:, :, cols, :].rearrange("p v m j -> p m j v"),
-                in_=wk_raw[piece][:].rearrange("p j (m u v) -> p u m j v", u=2, v=2)[:, u, src_cols],
+                out=wk_bf[u][:, :, cols, places].rearrange("p v m j -> p m j v"),
+                in_=wk_raw[:, places].rearrange("p j (m u v) -> p u m j v", u=2, v=2)[:, u, cols],
             )
 
-        def quantise_wk(h, u):
-            for v in range(2):
-                cols = slice(h * M_HALF, (h + 1) * M_HALF)
-                t = 2 * u + v
-                quantise(wk_codes[t][:, cols], wk_scales[t][:, cols], wk_bf[h][u][:, v].rearrange("p m j -> p (m j)"))
+        def quantise_wk(t):
+            quantise(wk_codes[t][:], wk_scales[t][:], wk_bf[t // 2][:, t % 2].rearrange("p m j -> p (m j)"))
 
-        low, high = slice(0, M_HALF // 2), slice(M_HALF // 2, M_HALF)
-        for piece, cols in enumerate((low, high)):
-            for u in range(2):
-                deal(nc.scalar.copy, piece, 0, u, cols, low)
-        by_scalar, by_vector = slice(0, M_SCALAR), slice(M_SCALAR, M_HALF)
+        deal(nc.scalar.copy, 0, slice(0, M_SCALAR[0]), slice(0, 1))
+        deal(nc.scalar.copy, 0, slice(0, M_SCALAR[0]), slice(1, PACK))
+        deal(nc.scalar.copy, 1, slice(0, M_SCALAR[1]))
         for u in range(2):
-            deal(nc.scalar.copy, 2, 1, u, by_scalar, by_scalar)
-        quantise_wk(0, 0)
-        quantise_wk(0, 1)
-        for u in range(2):
-            deal(nc.vector.tensor_copy, 2, 1, u, by_vector, by_vector)
-        quantise_wk(1, 0)
-        quantise_wk(1, 1)
+            deal(nc.vector.tensor_copy, u, slice(M_SCALAR[u], P))
+        quantise_wk(0)
+        quantise_wk(1)
         enc_w = [keep.tile([P, HALF], U16, name="enc_w0", align_bytes=64)]
         nc.vector.tensor_copy(enc_w[0][:], word_win[:].indirect(offsets[:, : HALF // 16]))
+        for t in range(2, PACK):
+            quantise_wk(t)
 
-        enc_w.append(reuse.tile([P, HALF], U16, name="enc_w1", align_bytes=64, offset=10240))
+        enc_w.append(reuse.tile([P, HALF], U16, name="enc_w1", align_bytes=64, offset=4096))
         nc.vector.tensor_copy(enc_w[1][:], word_win[:].indirect(offsets[:, HALF // 16 :]))
 
-        score_bf = reuse.tile([P, M, PACK], BF16, name="score_bf", align_bytes=64, offset=10752)
+        score_bf = reuse.tile([P, M, PACK], BF16, name="score_bf", align_bytes=64, offset=4608)
         score_codes = keep.tile([P, M], U32, name="score_codes", align_bytes=64)
         score_scales = keep.tile([P, M], U8, name="score_scales", align_bytes=64)
         nc.vector.tensor_copy(
@@ -200,10 +187,9 @@ def tile_attend_additiveattn_kernel(tc, enc_words, enc_scales, wk, qterm, gain, 
         )
         nc.scalar.activation(out=p_sb[:], in_=neg_a[:], func=ACT.Exp, bias=neg_max[:], scale=-1.0, accum_out=row_sum[:])
         nc.vector.reciprocal(out=inv_sum[:], in_=row_sum[:])
-        for h, (queue, lo, hi) in enumerate(((nc.sync, 0, 128), (nc.scalar, 128, 320), (nc.sync, 320, I))):
-            cols = slice(lo, hi)
+        for h, (queue, lo, hi) in enumerate(((nc.sync, 0, 128), (nc.scalar, 128, 256), (nc.sync, 256, I))):
             y_sb = keep.tile([M, hi - lo], F32, name="y_sb%d" % h, align_bytes=64)
             nc.vector.tensor_scalar(
-                out=y_sb[:], in0=p_sb[:, cols], scalar1=inv_sum[:], scalar2=512.0, op0=ALU.mult, op1=ALU.mult
+                out=y_sb[:], in0=p_sb[:, lo:hi], scalar1=inv_sum[:], scalar2=512.0, op0=ALU.mult, op1=ALU.mult
             )
-            queue.dma_start(out=out[:, cols], in_=y_sb[:])
+            queue.dma_start(out=out[:, lo:hi], in_=y_sb[:])

@@ -99,8 +99,9 @@ def tile_attend_additiveattn_kernel(tc, enc_words, enc_scales, wk, qterm, gain, 
             in_=score_raw[:].rearrange("p j (n e) -> p n j e", e=2),
         )
 
-        th = [keep.tile([P, PACK, CHUNK], F32, name="th%d" % c, align_bytes=64) for c in range(N_CHUNKS)]
-        h_bf = [keep.tile([P, CHUNK, PACK], BF16, name="h_bf%d" % c, tag="h_bf%d" % c, align_bytes=64) for c in range(N_CHUNKS)]
+        th = [keep.tile([P, PACK, CHUNK], F32, name="th%d" % c, tag="th%d" % c, align_bytes=64) for c in range(N_CHUNKS)]
+        h_bf = [reuse.tile([P, CHUNK, PACK], BF16, name="h_bf0", align_bytes=64, offset=0)]
+        h_bf.extend(keep.tile([P, CHUNK, PACK], BF16, name="h_bf%d" % c, tag="h_bf%d" % c, align_bytes=64) for c in range(1, N_CHUNKS))
         h_codes = [keep.tile([P, CHUNK], U32, name="h_codes%d" % c, align_bytes=64) for c in range(N_CHUNKS)]
         h_scales = [keep.tile([P, CHUNK], U8, name="h_scales%d" % c, align_bytes=64) for c in range(N_CHUNKS)]
         g_bc = g_col[:].rearrange("p (a t b) -> p a t b", a=1, b=1).broadcast_to([P, CHUNK // 2, PACK, 2])
@@ -148,8 +149,8 @@ def tile_attend_additiveattn_kernel(tc, enc_words, enc_scales, wk, qterm, gain, 
         for c, banks in ((1, (4, 5)), (2, (0, 1)), (3, (2, 3))):
             pair = [zps.tile([P, 2, CHUNK], F32, name="z_pair%d" % b, tag="bank%d" % b) for b in banks]
             project_and_tanh(c, [pair[t // 2][:, t % 2, :] for t in range(PACK)])
-        weigh(0)
         quantise(score_codes[:], score_scales[:], score_bf[:].rearrange("p m j -> p (m j)"))
+        weigh(0)
         last = N_CHUNKS - 1
         for c in range(1, last):
             weigh(c)
@@ -164,7 +165,7 @@ def tile_attend_additiveattn_kernel(tc, enc_words, enc_scales, wk, qterm, gain, 
         neg_max = keep.tile([M, 1], F32, name="neg_max")
         row_sum = keep.tile([M, 1], F32, name="row_sum")
         inv_sum = keep.tile([M, 1], F32, name="inv_sum")
-        neg_a = keep.tile([M, I], F32, name="neg_a", tag="h_bf2", align_bytes=64)
+        neg_a = keep.tile([M, I], F32, name="neg_a", tag="th3", align_bytes=64)
         p_sb = keep.tile([M, I], F32, name="p_sb", align_bytes=64)
 
         nc.vector.tensor_scalar(

@@ -156,7 +156,13 @@ def tile_attend_additiveattn_kernel(tc, enc_words, enc_scales, wk, qterm, gain, 
             weigh(c)
             quantise_and_score(c - 1)
         weigh(last, 0, CHUNK // 2)
-        weigh(last, CHUNK // 2, CHUNK)
+        tail = keep.tile([P, PACK, CHUNK // 2], F32, name="tail", tag="tail", align_bytes=64)
+        for t in range(PACK):
+            nc.scalar.activation(out=tail[:, t, :], in_=th[last][:, t, CHUNK // 2 :], func=ACT.Copy, scale=g_col[:, t : t + 1])
+        nc.vector.tensor_copy(
+            out=h_bf[last][:, CHUNK // 2 :].rearrange("p (n e) t -> p n t e", e=2),
+            in_=tail[:].rearrange("p t (n e) -> p n t e", e=2),
+        )
         quantise_and_score(last - 1)
         quantise_and_score(last, 0, CHUNK // 2)
         quantise_and_score(last, CHUNK // 2, CHUNK)
@@ -165,7 +171,7 @@ def tile_attend_additiveattn_kernel(tc, enc_words, enc_scales, wk, qterm, gain, 
         neg_max = keep.tile([M, 1], F32, name="neg_max")
         row_sum = keep.tile([M, 1], F32, name="row_sum")
         inv_sum = keep.tile([M, 1], F32, name="inv_sum")
-        neg_a = keep.tile([M, I], F32, name="neg_a", tag="th3", align_bytes=64)
+        neg_a = keep.tile([M, I], F32, name="neg_a", tag="tail", align_bytes=64)
         p_sb = keep.tile([M, I], F32, name="p_sb", align_bytes=64)
 
         nc.vector.tensor_scalar(

from contextlib import ExitStack

import concourse.mybir as mybir

K, T, I, F, M = 512, 2048, 512, 512, 128
FLOPS = 2 * K * F * I + 2 * F * M * I

F32 = mybir.dt.float32
BF16 = mybir.dt.bfloat16
I32 = mybir.dt.int32
U32 = mybir.dt.uint32
U16 = mybir.dt.uint16
U8 = mybir.dt.uint8
FP8X4 = mybir.dt.float8_e4m3fn_x4
FP4X4 = mybir.dt.float4_e2m1fn_x4
ACT = mybir.ActivationFunctionType
ALU = mybir.AluOpType

P = 128
PACK = 4
QUADRANT = 32
HALF = I // 2
CHUNK = 128
N_CHUNKS = I // CHUNK
M_SCALAR = (42, 96)


def tile_attend_additiveattn_kernel(tc, enc_words, enc_scales, wk, qterm, gain, score, offs, out):
    nc = tc.nc
    with ExitStack() as ctx:
        keep = ctx.enter_context(tc.tile_pool(name="keep", bufs=1))
        reuse = ctx.enter_context(tc.tile_pool(name="reuse", bufs=1))
        zps = ctx.enter_context(tc.psum_pool(name="zps", bufs=1))
        aps = ctx.enter_context(tc.psum_pool(name="aps", bufs=1))

        def quantise(codes, scales, values):
            nc.vector.quantize_mx(out=codes.bitcast(FP8X4), scales=scales, in_=values)

        offsets = keep.tile([P, I // 16], U16, name="offsets")
        scale_win = reuse.tile([P, T], U8, name="scale_win", align_bytes=64, offset=0)
        word_win = keep.tile([P, T], U16, name="word_win", align_bytes=64)
        wk_raw = keep.tile([P, PACK, F], F32, name="wk_raw", align_bytes=64)
        q_col = keep.tile([P, PACK], F32, name="q_col")
        g_col = keep.tile([P, PACK], F32, name="g_col")
        enc_s = keep.tile([P, I], U8, name="enc_s", align_bytes=64)

        nc.vector.memset(scale_win[:].bitcast(I32), 0)
        nc.vector.memset(enc_s[:].bitcast(I32), 0)
        wk_rows = wk.rearrange("(p j) f -> p j f", j=PACK)
        nc.sync.dma_start(out=wk_raw[:, :1], in_=wk_rows[:, :1])
        nc.sync.dma_start(offsets[:], offs)
        nc.sync.dma_start(out=scale_win[0:P:8, :].bitcast(I32), in_=enc_scales[0].bitcast(I32))
        nc.sync.dma_start(out=wk_raw[:, 1:2], in_=wk_rows[:, 1:2])
        nc.sync.dma_start(out=wk_raw[:, 2:], in_=wk_rows[:, 2:])
        nc.sync.dma_start(out=word_win[:].bitcast(I32), in_=enc_words[0].bitcast(I32))
        nc.sync.dma_start(out=q_col[:], in_=qterm.rearrange("(p t) o -> p (t o)", t=PACK))
        nc.sync.dma_start(out=g_col[:], in_=gain.rearrange("(p t) o -> p (t o)", t=PACK))

        spread_s = keep.tile([P, I], U8, name="spread_s", align_bytes=64)
        nc.vector.tensor_copy(spread_s[:], scale_win[:].indirect(offsets[:]))
        for r in range(4):
            nc.sync.dma_start(out=enc_s[r:P:QUADRANT, :].bitcast(I32), in_=spread_s[8 * r : P : QUADRANT, :].bitcast(I32))
        score_raw = reuse.tile([P, PACK, M], F32, name="score_raw", align_bytes=64, offset=0)
        nc.sync.dma_start(out=score_raw[:], in_=score.rearrange("(p j) m -> p j m", j=PACK))

        wk_codes = [keep.tile([P, P], U32, name="wk_codes%d" % t, align_bytes=64) for t in range(PACK)]
        wk_scales = [keep.tile([P, P], U8, name="wk_scales%d" % t, align_bytes=64) for t in range(PACK)]
        wk_bf = [reuse.tile([P, 2, P, PACK], BF16, name="wk_bf%d" % u, align_bytes=64, offset=2048 * (1 + u)) for u in range(2)]

        def deal(copy, u, cols, places=slice(0, PACK)):
            copy(
                out=wk_bf[u][:, :, cols, places].rearrange("p v m j -> p m j v"),
                in_=wk_raw[:, places].rearrange("p j (m u v) -> p u m j v", u=2, v=2)[:, u, cols],
            )

        def quantise_wk(t):
            quantise(wk_codes[t][:], wk_scales[t][:], wk_bf[t // 2][:, t % 2].rearrange("p m j -> p (m j)"))

        deal(nc.scalar.copy, 0, slice(0, M_SCALAR[0]), slice(0, 1))
        deal(nc.scalar.copy, 0, slice(0, M_SCALAR[0]), slice(1, PACK))
        deal(nc.scalar.copy, 1, slice(0, M_SCALAR[1]))
        for u in range(2):
            deal(nc.vector.tensor_copy, u, slice(M_SCALAR[u], P))
        quantise_wk(0)
        quantise_wk(1)
        enc_w = [keep.tile([P, HALF], U16, name="enc_w0", align_bytes=64)]
        nc.vector.tensor_copy(enc_w[0][:], word_win[:].indirect(offsets[:, : HALF // 16]))
        for t in range(2, PACK):
            quantise_wk(t)

        enc_w.append(reuse.tile([P, HALF], U16, name="enc_w1", align_bytes=64, offset=4096))
        nc.vector.tensor_copy(enc_w[1][:], word_win[:].indirect(offsets[:, HALF // 16 :]))

        score_bf = reuse.tile([P, M, PACK], BF16, name="score_bf", align_bytes=64, offset=4608)
        score_codes = keep.tile([P, M], U32, name="score_codes", align_bytes=64)
        score_scales = keep.tile([P, M], U8, name="score_scales", align_bytes=64)
        nc.vector.tensor_copy(
            out=score_bf[:].rearrange("p (n e) j -> p n j e", e=2),
            in_=score_raw[:].rearrange("p j (n e) -> p n j e", e=2),
        )

        th = [keep.tile([P, PACK, CHUNK], F32, name="th%d" % c, tag="th%d" % c, align_bytes=64) for c in range(N_CHUNKS)]
        h_bf = [reuse.tile([P, CHUNK, PACK], BF16, name="h_bf0", align_bytes=64, offset=0)]
        h_bf.extend(keep.tile([P, CHUNK, PACK], BF16, name="h_bf%d" % c, tag="h_bf%d" % c, align_bytes=64) for c in range(1, N_CHUNKS))
        h_codes = [keep.tile([P, CHUNK], U32, name="h_codes%d" % c, align_bytes=64) for c in range(N_CHUNKS)]
        h_scales = [keep.tile([P, CHUNK], U8, name="h_scales%d" % c, align_bytes=64) for c in range(N_CHUNKS)]
        g_bc = g_col[:].rearrange("p (a t b) -> p a t b", a=1, b=1).broadcast_to([P, CHUNK // 2, PACK, 2])
        a_early = aps.tile([M, HALF], F32, name="a_early")
        a_last = aps.tile([M, HALF], F32, name="a_last")

        def project_and_tanh(c, z):
            h, lo = divmod(c * CHUNK, HALF)
            for t in range(PACK):
                nc.tensor.matmul_mx(
                    out=z[t],
                    lhsT=wk_codes[t][:].bitcast(FP8X4),
                    lhsT_scale=wk_scales[t][:],
                    rhs=enc_w[h][:, lo : lo + CHUNK].bitcast(FP4X4),
                    rhs_scale=enc_s[:, c * CHUNK : (c + 1) * CHUNK],
                    start=True,
                    stop=True,
                )
            for t in range(PACK):
                nc.scalar.activation(
                    out=th[c][:, t, :], in_=z[t], func=ACT.Tanh, bias=q_col[:, t : t + 1], scale=1.0
                )

        def weigh(c, lo=0, hi=CHUNK):
            nc.vector.tensor_tensor(
                out=h_bf[c][:, lo:hi].rearrange("p (n e) t -> p n t e", e=2),
                in0=th[c][:, :, lo:hi].rearrange("p t (n e) -> p n t e", e=2),
                in1=g_bc[:, : (hi - lo) // 2],
                op=ALU.mult,
            )

        def quantise_and_score(c, lo=0, hi=CHUNK):
            quantise(h_codes[c][:, lo:hi], h_scales[c][:, lo:hi], h_bf[c][:, lo:hi].rearrange("p n t -> p (n t)"))
            nc.tensor.matmul_mx(
                out=(a_early, a_last)[c // 2][:, (c % 2) * CHUNK + lo : (c % 2) * CHUNK + hi],
                lhsT=score_codes[:].bitcast(FP8X4),
                lhsT_scale=score_scales[:],
                rhs=h_codes[c][:, lo:hi].bitcast(FP8X4),
                rhs_scale=h_scales[c][:, lo:hi],
                start=True,
                stop=True,
            )

        project_and_tanh(0, [zps.tile([P, CHUNK], F32, name="z%d" % t, tag="bank%d" % t)[:] for t in range(PACK)])
        for c, banks in ((1, (4, 5)), (2, (0, 1)), (3, (2, 3))):
            pair = [zps.tile([P, 2, CHUNK], F32, name="z_pair%d" % b, tag="bank%d" % b) for b in banks]
            project_and_tanh(c, [pair[t // 2][:, t % 2, :] for t in range(PACK)])
        quantise(score_codes[:], score_scales[:], score_bf[:].rearrange("p m j -> p (m j)"))
        weigh(0)
        last = N_CHUNKS - 1
        for c in range(1, last):
            weigh(c)
            quantise_and_score(c - 1)
        weigh(last, 0, CHUNK // 2)
        tail = keep.tile([P, PACK, CHUNK // 2], F32, name="tail", tag="tail", align_bytes=64)
        for t in range(PACK):
            nc.scalar.activation(out=tail[:, t, :], in_=th[last][:, t, CHUNK // 2 :], func=ACT.Copy, scale=g_col[:, t : t + 1])
        nc.vector.tensor_copy(
            out=h_bf[last][:, CHUNK // 2 :].rearrange("p (n e) t -> p n t e", e=2),
            in_=tail[:].rearrange("p t (n e) -> p n t e", e=2),
        )
        quantise_and_score(last - 1)
        quantise_and_score(last, 0, CHUNK // 2)
        quantise_and_score(last, CHUNK // 2, CHUNK)

        neg_max_early = keep.tile([M, 1], F32, name="neg_max_early")
        neg_max = keep.tile([M, 1], F32, name="neg_max")
        row_sum = keep.tile([M, 1], F32, name="row_sum")
        inv_sum = keep.tile([M, 1], F32, name="inv_sum")
        neg_a = keep.tile([M, I], F32, name="neg_a", tag="tail", align_bytes=64)
        p_sb = keep.tile([M, I], F32, name="p_sb", align_bytes=64)

        nc.vector.tensor_scalar(
            out=neg_a[:, :HALF],
            in0=a_early[:],
            scalar1=-1.0,
            scalar2=None,
            op0=ALU.mult,
            op1=ALU.min,
            accum_out=neg_max_early[:],
        )
        nc.vector.tensor_scalar(
            out=neg_a[:, HALF:],
            in0=a_last[:],
            scalar1=-1.0,
            scalar2=neg_max_early[:],
            op0=ALU.mult,
            op1=ALU.min,
            accum_out=neg_max[:],
        )
        nc.scalar.activation(out=p_sb[:], in_=neg_a[:], func=ACT.Exp, bias=neg_max[:], scale=-1.0, accum_out=row_sum[:])
        nc.vector.reciprocal(out=inv_sum[:], in_=row_sum[:])
        for h, (queue, lo, hi) in enumerate(((nc.sync, 0, 128), (nc.scalar, 128, 256), (nc.sync, 256, I))):
            y_sb = keep.tile([M, hi - lo], F32, name="y_sb%d" % h, align_bytes=64)
            nc.vector.tensor_scalar(
                out=y_sb[:], in0=p_sb[:, lo:hi], scalar1=inv_sum[:], scalar2=512.0, op0=ALU.mult, op1=ALU.mult
            )
            queue.dma_start(out=out[:, lo:hi], in_=y_sb[:])
